import numpy as np
import ml_dtypes


def mxq(x, axis, fmt="e4m3"):
    dtype, down = {"e4m3": (ml_dtypes.float8_e4m3fn, 7), "e5m2": (ml_dtypes.float8_e5m2, 14)}[fmt]
    v = np.moveaxis(np.asarray(x, np.float32).astype(ml_dtypes.bfloat16).astype(np.float64), axis, -1)
    blocks = v.reshape(v.shape[:-1] + (-1, 32))
    amax = np.abs(blocks).max(-1, keepdims=True)
    byte = np.maximum(np.where(amax > 0, np.frexp(amax)[1] - 1 + 127, 0) - down, 1)
    scale = np.exp2(byte - 127.0)
    codes = (blocks / scale).astype(np.float32).astype(dtype).astype(np.float64)
    return np.moveaxis((codes * scale).reshape(v.shape), -1, axis)


WIDE = False


def mx_kscale(k):
    if not WIDE:
        return np.ones(k)
    levels = np.array([10, -10, 5, -5, 0])
    if k % 512:
        return np.exp2(np.random.permutation(np.resize(levels, k // 32))).repeat(32)
    a = np.empty((k // 512, 16))
    for p in range(k // 512):
        a[p, :8] = np.random.permutation(np.resize(levels, 8))
        for g in range(8):
            far = levels[np.abs(levels - a[p, g]) >= 10]
            a[p, g + 8] = far[np.random.randint(len(far))]
    return np.exp2(a.ravel()).repeat(32)


def f64(x):
    return np.asarray(x).astype(np.float64)


def striped(idx):
    return np.tile(idx.reshape(-1, 16).T, (8, 1)).astype(np.uint16)


def unstriped(offs):
    return offs[:16].T.reshape(-1).astype(np.int64)


E2M1 = np.array([0.0, 0.5, 1.0, 1.5, 2.0, 3.0, 4.0, 6.0, -0.0, -0.5, -1.0, -1.5, -2.0, -3.0, -4.0, -6.0])


def pack_weight(w, fmt):
    k, n = w.shape
    w = f64(np.asarray(w, np.float32).astype(ml_dtypes.bfloat16)).reshape(k // 32, 32, n)
    amax = np.abs(w).max(1)
    if fmt == "e4m3":
        byte = np.frexp(amax)[1] - 1 + 127 - 7
    else:
        mant, ex = np.frexp(amax / 6.0)
        byte = np.where(mant > 0.5, ex, ex - 1) + 127
    byte = np.clip(np.where(amax > 0, byte, 1), 1, 254)
    scaled = (w * np.exp2(127.0 - byte)[:, None, :]).reshape(k, n).astype(np.float32)
    by_word = np.ascontiguousarray(scaled.reshape(k // 512, 128, 4, n).transpose(0, 1, 3, 2))
    if fmt == "e4m3":
        words = by_word.astype(ml_dtypes.float8_e4m3fn).view(np.uint8)
    else:
        c = by_word.astype(ml_dtypes.float4_e2m1fn).view(np.uint8) & 0xF
        words = (c[..., 0::2] | (c[..., 1::2] << 4)).reshape(k // 512, 128, 2 * n)
    return np.ascontiguousarray(words), np.ascontiguousarray(byte.astype(np.uint8).reshape(k // 512, 16, n))


def unpack_weight(words, scales, fmt):
    g, _, n = scales.shape
    words = np.ascontiguousarray(words).reshape(g, 128, n, -1)
    if fmt == "e4m3":
        vals = words.view(ml_dtypes.float8_e4m3fn).astype(np.float64)
    else:
        nib = np.empty((g, 128, n, 4), np.uint8)
        nib[..., 0::2] = words & 0xF
        nib[..., 1::2] = words >> 4
        vals = E2M1[nib]
    vals = vals * np.repeat(np.exp2(scales.astype(np.float64) - 127.0), 8, axis=1)[..., None]
    return vals.transpose(0, 1, 3, 2).reshape(g * 512, n)


def gelu(v):
    return 0.5 * v * (1.0 + np.tanh(np.sqrt(2.0 / np.pi) * (v + 0.044715 * v**3)))


K, T, S, M, H, T2, P, N = 1024, 2048, 512, 512, 1024, 2048, 1024, 512

def setup_inputs():
    n = np.random.standard_normal
    s = mx_kscale(K)[:, None]
    u = mx_kscale(M)[:, None]
    w = mx_kscale(H)[:, None]
    perm = np.random.permutation(T2)
    d = {}
    d["tab_words"], d["tab_scales"] = pack_weight(n((K, T)) * s, "e4m3")
    d["tab2_words"], d["tab2_scales"] = pack_weight(n((K, T)) * s, "e4m3")
    d["offs"] = striped(np.random.permutation(T)[:S])
    d["offs2"] = striped(np.random.permutation(T)[:S])
    d["offs3"] = striped(perm[:S])
    d["offs4"] = striped(perm[S:2 * S])
    d["offs5"] = striped(np.random.permutation(T2)[:P])
    d["w1"] = (n((K, M)) / s * u.T / K ** 0.5).astype(np.float32)
    d["w2_words"], d["w2_scales"] = pack_weight(n((K, M)) / s / K ** 0.5, "e2m1")
    d["ref"] = (0.7 * n(M) * u[:, 0]).astype(np.float32)
    d["w3"] = (n((M, H)) / u * w.T / M ** 0.5).astype(np.float32)
    d["w4"] = (n((K, H)) / s * w.T / K ** 0.5).astype(np.float32)
    d["page0"] = (n((H, T2)) * w).astype(np.float32)
    d["wg1"] = np.exp(0.3 * n((128, S))).astype(np.float32)
    d["wg2"] = np.exp(0.3 * n((128, S))).astype(np.float32)
    d["vec"] = (n(H) * w[:, 0]).astype(np.float32)
    d["w5_words"], d["w5_scales"] = pack_weight(n((H, N)) / w / H ** 0.5, "e2m1")
    return d

def reference(tab_words, tab_scales, tab2_words, tab2_scales, offs, offs2, offs3, offs4, offs5, w1, w2_words, w2_scales, ref, w3, w4, page0, wg1, wg2, vec, w5_words, w5_scales):
    v = unpack_weight(tab_words, tab_scales, "e4m3")[:, unstriped(offs)]
    v2 = unpack_weight(tab2_words, tab2_scales, "e4m3")[:, unstriped(offs2)]
    a = mxq(f64(w1), 0, "e4m3").T @ v
    b = unpack_weight(w2_words, w2_scales, "e2m1").T @ v
    f = a * b - f64(ref)[:, None]
    h1 = mxq(f64(w3), 0, "e4m3").T @ mxq(f, 0, "e4m3")
    h2 = np.abs(mxq(f64(w4), 0, "e4m3").T @ v2)
    page = f64(page0).copy()
    page[:, unstriped(offs3)] = np.tile(f64(wg1), (H // 128, 1)) * h1
    page[:, unstriped(offs4)] = np.tile(f64(wg2), (H // 128, 1)) * h2
    x = page[:, unstriped(offs5)] + f64(vec)[:, None]
    return unpack_weight(w5_words, w5_scales, "e2m1").T @ mxq(x, 0, "e4m3")

@@ -1,0 +1,377 @@
+from contextlib import ExitStack
+
+import concourse.mybir as mybir
+from concourse.masks import make_identity
+
+K, T, S, M, H, T2, NPICK, N = 1024, 2048, 512, 512, 1024, 2048, 1024, 512
+FLOPS = 2 * (2 * K * M * S + M * H * S + K * H * S + H * N * NPICK)
+
+F32 = mybir.dt.float32
+BF16 = mybir.dt.bfloat16
+I32 = mybir.dt.int32
+U32 = mybir.dt.uint32
+U16 = mybir.dt.uint16
+U8 = mybir.dt.uint8
+FP8X4 = mybir.dt.float8_e4m3fn_x4
+FP4X4 = mybir.dt.float4_e2m1fn_x4
+ACT = mybir.ActivationFunctionType
+ALU = mybir.AluOpType
+
+P = 128
+PACK = 4
+KP = P * PACK
+BANK = 512
+
+
+def tile_list_gem_tray_scores_kernel(
+    tc, tab_words, tab_scales, tab2_words, tab2_scales, offs, offs2, offs3, offs4, offs5,
+    w1, w2_words, w2_scales, ref, w3, w4, page0, wg1, wg2, vec, w5_words, w5_scales, out,
+):
+    nc = tc.nc
+    with ExitStack() as ctx:
+        lists = ctx.enter_context(tc.tile_pool(name="lists", bufs=1))
+        keep = ctx.enter_context(tc.tile_pool(name="keep", bufs=1))
+        big = ctx.enter_context(tc.tile_pool(name="big", bufs=6))
+        rows = ctx.enter_context(tc.tile_pool(name="rows", bufs=10))
+        half = ctx.enter_context(tc.tile_pool(name="half", bufs=4))
+        psum = ctx.enter_context(tc.psum_pool(name="psum", bufs=8))
+
+        def bank():
+            return psum.tile([P, BANK], F32, name="bank")
+
+        def row_tile():
+            return rows.tile([P, S], F32, name="row")
+
+        def load_list(src, name):
+            t = lists.tile([P, src.shape[1]], U16, name=name)
+            nc.sync.dma_start(t[:], src)
+            return t
+
+        def zeroed_plane(shape, name):
+            t = keep.tile(shape, U8, name=name, align_bytes=64)
+            nc.vector.memset(t[:].bitcast(I32), 0)
+            return t
+
+        def load_planes_side_by_side(queue, plane, src, quadrants=(0, 2, 1, 3)):
+            for q in quadrants:
+                queue.dma_start(
+                    out=plane[32 * q : 32 * q + 4, :].bitcast(I32).rearrange("r (a c) -> r a c", a=2),
+                    in_=src[:, 4 * q : 4 * q + 4, :].bitcast(I32).rearrange("a r c -> r a c"),
+                )
+
+        def load_words(src, a):
+            t = big.tile([P, T], U32, name="big", align_bytes=64)
+            nc.sync.dma_start(out=t[:].bitcast(I32), in_=src[a].rearrange("p n i -> p (n i)").bitcast(I32))
+            return t
+
+        def gather(src, idx, dtype, name):
+            t = keep.tile([P, S], dtype, name=name, align_bytes=64)
+            nc.vector.tensor_copy(t[:], src.indirect(idx[:]))
+            return t
+
+        def load_weight(w, a, g):
+            t = big.tile([P, PACK, KP], F32, name="big", align_bytes=64)
+            nc.sync.dma_start(
+                out=t[:],
+                in_=w[KP * a : KP * (a + 1), KP * g : KP * (g + 1)].rearrange("(p i) c -> p i c", i=PACK),
+            )
+            return t
+
+        def round_weight(copy, raw, t=None):
+            if t is None:
+                t = half.tile([P, PACK * KP], BF16, name="half", align_bytes=64)
+            copy(
+                out=t[:].rearrange("p (t m i) -> p m t i", t=PACK, i=PACK),
+                in_=raw[:].rearrange("p i (m t) -> p m t i", t=PACK),
+            )
+            return t
+
+        def quantize(src, width, name):
+            codes = keep.tile([P, width], U32, name=name + "_codes", align_bytes=64)
+            scales = keep.tile([P, width], U8, name=name + "_scales", align_bytes=64)
+            nc.vector.quantize_mx(out=codes[:].bitcast(FP8X4), scales=scales[:], in_=src)
+            return codes, scales
+
+        def load_page(g, t):
+            pg = keep.tile([P, T2], F32, name="page%d_%d" % (g, t))
+            nc.sync.dma_start(
+                out=pg[:], in_=page0[KP * g : KP * (g + 1), :].rearrange("(p t) c -> t p c", t=PACK)[t]
+            )
+            return pg
+
+        def load_gain(wg):
+            t = row_tile()
+            nc.sync.dma_start(out=t[:], in_=wg)
+            return t
+
+        def deal_gain(natural, name):
+            turned = keep.tile([P, PACK, BANK], F32, name="turned")
+            for c in range(PACK):
+                b = bank()
+                for q in range(4):
+                    nc.tensor.transpose(b[:, P * q : P * (q + 1)], natural[:, P * c : P * (c + 1)], ident[:])
+                nc.scalar.copy(
+                    out=turned[:, c, :].rearrange("j (t p) -> j t p", t=PACK),
+                    in_=b[:].rearrange("j (p t) -> j t p", t=PACK),
+                )
+            dealt = []
+            for t in range(PACK):
+                b = bank()
+                for c in range(PACK):
+                    nc.tensor.transpose(b[:, P * c : P * (c + 1)], turned[:, c, P * t : P * (t + 1)], ident[:])
+                d = keep.tile([P, S], F32, name="%s%d" % (name, t))
+                nc.scalar.copy(out=d[:], in_=b[:])
+                dealt.append(d)
+            return dealt
+
+        def mx(acc, lhs, lhs_scale, lhs_dtype, rhs, rhs_scale, start, stop, rhs_dtype=FP8X4):
+            nc.tensor.matmul_mx(
+                out=acc, lhsT=lhs.bitcast(lhs_dtype), lhsT_scale=lhs_scale,
+                rhs=rhs.bitcast(rhs_dtype), rhs_scale=rhs_scale, start=start, stop=stop,
+            )
+
+        def scatter(pg, idx, h, gain):
+            nc.vector.tensor_tensor(pg[:].indirect(idx[:]), h, gain[:], ALU.mult)
+
+        ident = keep.tile([P, P], F32, name="ident")
+        make_identity(nc, ident[:])
+        tab2_plane = zeroed_plane([P, T], "tab2_plane")
+        tab_plane = zeroed_plane([P, 2 * T], "tab_plane")
+        w2_plane = zeroed_plane([P, 2 * M], "w2_plane")
+        w5_plane = zeroed_plane([P, 2 * N], "w5_plane")
+
+        def load_packed_planes(quadrants):
+            for q in quadrants:
+                nc.sync.dma_start(
+                    out=tab2_plane[32 * q : 32 * q + 8, :].bitcast(I32),
+                    in_=tab2_scales[:, 4 * q : 4 * q + 4, :].bitcast(I32),
+                )
+
+        wg2_nat = load_gain(wg2)
+        idx2 = load_list(offs2, "idx2")
+        idx1 = load_list(offs, "idx1")
+        idx4 = load_list(offs4, "idx4")
+        idx3 = load_list(offs3, "idx3")
+        idx5 = load_list(offs5, "idx5")
+        tab2_w0 = load_words(tab2_words, 0)
+        load_packed_planes((0, 2, 1, 3))
+        w4_raw00 = load_weight(w4, 0, 0)
+        load_planes_side_by_side(nc.sync, tab_plane, tab_scales)
+        w4_raw10 = load_weight(w4, 1, 0)
+        tab2_w1 = load_words(tab2_words, 1)
+        pages = {}
+        pages[0, 0] = load_page(0, 0)
+
+        ref_col = keep.tile([P, PACK], F32, name="ref_col")
+        nc.gpsimd.dma_start(out=ref_col[:], in_=ref.rearrange("(p t) -> p t", t=PACK))
+        load_planes_side_by_side(nc.gpsimd, w2_plane, w2_scales)
+        vec_col = keep.tile([P, 2, PACK], F32, name="vec_col")
+        nc.gpsimd.dma_start(out=vec_col[:], in_=vec.rearrange("(g p t) -> p g t", g=2, t=PACK))
+        load_planes_side_by_side(nc.gpsimd, w5_plane, w5_scales)
+
+        gain2 = deal_gain(wg2_nat, "gain2_")
+        v2 = [gather(tab2_w0[:], idx2, U32, "v2_0")]
+        v2_scales = gather(tab2_plane[:], idx2, U8, "v2_scales")
+        w4q = {}
+        w4q[0, 0] = quantize(round_weight(nc.vector.tensor_copy, w4_raw00)[:], KP, "w4_00")
+        v_scales = [gather(tab_plane[:, T * a : T * (a + 1)], idx1, U8, "v_scales%d" % a) for a in range(2)]
+        w4q[1, 0] = quantize(round_weight(nc.scalar.copy, w4_raw10)[:], KP, "w4_10")
+        v2.append(gather(tab2_w1[:], idx2, U32, "v2_1"))
+
+        ref_bank = bank()
+        for t in range(PACK):
+            nc.tensor.transpose(ref_bank[:, P * t : P * (t + 1)], ref_col[:, t : t + 1].to_broadcast([P, P]), ident[:])
+        neg_ref = keep.tile([P, M], F32, name="neg_ref")
+        nc.scalar.activation(out=neg_ref[:], in_=ref_bank[:], func=ACT.Identity, scale=-1.0)
+
+        def h2_sums(g, t):
+            b = bank()
+            cols = slice(P * t, P * (t + 1))
+            for a in range(2):
+                codes, scales = w4q[a, g]
+                mx(b[:], codes[:, cols], scales[:, cols], FP8X4, v2[a][:], v2_scales[4 * a : P, :], a == 0, a == 1)
+            return b
+
+        def h2_rows(g, t):
+            h = row_tile()
+            nc.scalar.activation(out=h[:], in_=h2_sums(g, t)[:], func=ACT.Abs)
+            return h[:]
+
+        wg1_nat = load_gain(wg1)
+        pages[0, 1] = load_page(0, 1)
+        w4_raw01 = load_weight(w4, 0, 1)
+        pages[0, 2] = load_page(0, 2)
+        w4_raw11 = load_weight(w4, 1, 1)
+        pages[0, 3] = load_page(0, 3)
+        w2_w = keep.tile([P, 2, 2 * M], U8, name="w2_w", align_bytes=64)
+        nc.sync.dma_start(out=w2_w[:].bitcast(I32), in_=w2_words.bitcast(I32).rearrange("a p c -> p a c"))
+        tab_w0 = load_words(tab_words, 0)
+        pages[1, 0] = load_page(1, 0)
+        tab_w1 = load_words(tab_words, 1)
+        w1_raw0 = load_weight(w1, 0, 0)
+        pages[1, 1] = load_page(1, 1)
+        pages[1, 2] = load_page(1, 2)
+        w1_raw1 = load_weight(w1, 1, 0)
+        w3_raw0 = load_weight(w3, 0, 0)
+        pages[1, 3] = load_page(1, 3)
+        w3_raw1 = load_weight(w3, 0, 1)
+        w5_w = keep.tile([P, 2, 2 * N], U8, name="w5_w", align_bytes=64)
+        nc.sync.dma_start(out=w5_w[:].bitcast(I32), in_=w5_words.bitcast(I32).rearrange("a p c -> p a c"))
+
+        for t in range(PACK):
+            scatter(pages[0, t], idx4, h2_rows(0, t), gain2[t])
+        gain1 = deal_gain(wg1_nat, "gain1_")
+        for a, raw in enumerate((w4_raw01, w4_raw11)):
+            w4q[a, 1] = quantize(round_weight(nc.scalar.copy, raw)[:], KP, "w4_%d1" % a)
+        h2_late = [h2_rows(1, t) for t in range(PACK - 1)]
+        h2_last = h2_sums(1, PACK - 1)
+
+        def scatter_last_half(u, spent):
+            cols = slice(S // 2 * u, S // 2 * (u + 1))
+            nc.scalar.activation(out=spent[:, cols], in_=h2_last[:, cols], func=ACT.Abs)
+            nc.vector.tensor_tensor(
+                pages[1, 3][:].indirect(idx4[:, 16 * u : 16 * (u + 1)]), spent[:, cols], gain2[3][:, cols], ALU.mult
+            )
+
+        scatter(pages[1, 0], idx4, h2_late[0], gain2[0])
+
+        v = []
+        w1q = []
+        for a, (words, raw) in enumerate(((tab_w0, w1_raw0), (tab_w1, w1_raw1))):
+            v.append(gather(words[:], idx1, U32, "v_%d" % a))
+            w1q.append(quantize(round_weight(nc.scalar.copy, raw)[:], KP, "w1_%d" % a))
+        scatter(pages[1, 1], idx4, h2_late[1], gain2[1])
+        scatter(pages[1, 2], idx4, h2_late[2], gain2[2])
+
+        f_half = half.tile([P, S, PACK], BF16, name="half", align_bytes=64)
+        b_rows = []
+        for c in range(PACK):
+            bb = bank()
+            cols = slice(P * c, P * (c + 1))
+            for a in range(2):
+                mx(bb[:], v[a][:, cols], v_scales[a][:, cols], FP8X4,
+                   w2_w[:, a, :], w2_plane[:, M * a : M * (a + 1)], a == 0, a == 1, FP4X4)
+            b_sb = row_tile()
+            nc.scalar.copy(
+                out=b_sb[:].rearrange("j (t p) -> j t p", t=PACK), in_=bb[:].rearrange("j (p t) -> j t p", t=PACK)
+            )
+            b_rows.append(b_sb)
+        for c in range(PACK):
+            ba = bank()
+            cols = slice(P * c, P * (c + 1))
+            for a in range(2):
+                codes, scales = w1q[a]
+                mx(ba[:], v[a][:, cols], v_scales[a][:, cols], FP8X4, codes[:], scales[:], a == 0, a == 1)
+            prod = row_tile()
+            nc.vector.tensor_tensor(prod[:], ba[:], b_rows[c][:], ALU.mult)
+            fb = bank()
+            for u, term in enumerate((prod, neg_ref)):
+                for t in range(PACK):
+                    nc.tensor.matmul(
+                        fb[:, P * t : P * (t + 1)], term[:, P * t : P * (t + 1)], ident[:],
+                        start=(u == 0 and t == 0), stop=(u == 1 and t == PACK - 1), is_transpose=True,
+                    )
+            nc.scalar.copy(out=f_half[:, cols, :], in_=fb[:].rearrange("p (t j) -> p j t", t=PACK))
+        scatter_last_half(0, b_rows[0])
+        w3q = [quantize(round_weight(nc.scalar.copy, w3_raw0)[:], KP, "w3_0")]
+        f_codes, f_scales = quantize(f_half[:].rearrange("p j t -> p (j t)"), S, "f")
+        scatter_last_half(1, neg_ref)
+
+        x_codes = [[keep.tile([P, S], U32, name="x_codes%d%d" % (g, u), align_bytes=64) for u in range(2)] for g in range(2)]
+        x_scales = keep.tile([P, 2, NPICK], U8, name="x_scales", align_bytes=64)
+
+        def h1_rows(g, t, h):
+            b = bank()
+            cols = slice(P * t, P * (t + 1))
+            codes, scales = w3q[g]
+            mx(b[:], codes[:, cols], scales[:, cols], FP8X4, f_codes[:], f_scales[:], True, True)
+            nc.scalar.copy(out=h, in_=b[:])
+            return h
+
+        h1_sb = keep.tile([P, S], F32, name="h1_sb")
+
+        def pick(g, t, x_half, j0, j1, picked):
+            nc.vector.tensor_copy(picked, pages[g, t][:].indirect(idx5[:, j0 // 16 : j1 // 16]))
+            for lo in range(j0, j1, S):
+                hi = min(lo + S, j1)
+                nc.scalar.activation(
+                    out=x_half[lo // S][:, lo % S : lo % S + hi - lo, t], in_=picked[:, lo - j0 : hi - j0],
+                    func=ACT.Identity, bias=vec_col[:, g, t : t + 1],
+                )
+
+        def pick_all(g, t, x_half):
+            picked = big.tile([P, NPICK], F32, name="big", align_bytes=64)
+            pick(g, t, x_half, 0, NPICK, picked[:])
+
+        def quantize_x(g, x_half, j0, j1):
+            cols = slice(j0 % S, j0 % S + j1 - j0)
+            src = x_half[j0 // S][:, cols, :].rearrange("p j t -> p (j t)")
+            nc.vector.quantize_mx(out=x_codes[g][j0 // S][:, cols].bitcast(FP8X4), scales=x_scales[:, g, j0:j1], in_=src)
+
+        x0 = [half.tile([P, S, PACK], BF16, name="half", align_bytes=64) for u in range(2)]
+        w3_late = half.tile([P, PACK * KP], BF16, name="half", align_bytes=64)
+        x1 = [half.tile([P, S, PACK], BF16, name="half", align_bytes=64) for u in range(2)]
+        order = [(g, t) for g in range(2) for t in range(PACK)]
+        h1_other = keep.tile([P, S], F32, name="h1_other")
+        h = {0: h1_rows(0, 0, w3_late[:].bitcast(F32)[:, 0:S]), 1: h1_rows(0, 1, h1_other[:])}
+
+        def put(i):
+            g, t = order[i]
+            scatter(pages[g, t], idx3, h[i], gain1[t])
+
+        def fetch(i):
+            g, t = order[i]
+            pick_all(g, t, (x0, x1)[g])
+
+        for i in (0, 2, 4):
+            put(i)
+            h[i + 2] = h1_rows(*order[i + 2], h1_sb[:])
+            put(i + 1)
+            if i < 4:
+                h[i + 3] = h1_rows(*order[i + 3], h1_other[:])
+            if i == 0:
+                w3q.append(quantize(round_weight(nc.scalar.copy, w3_raw1, w3_late)[:], KP, "w3_1"))
+            fetch(i)
+            fetch(i + 1)
+        put(6)
+        h[7] = h1_rows(*order[7], h1_sb[:])
+        quantize_x(0, x0, 0, S)
+        fetch(6)
+        put(7)
+        quantize_x(0, x0, S, 2 * S)
+
+        CH = 256
+        acc = [[bank() for n2 in range(2)] for c in range(4)]
+
+        def final_passes(g, c):
+            for n2 in range(2):
+                for e in range(4):
+                    n, j0 = 2 * n2 + e // 2, CH * c + P * (e % 2)
+                    mx(acc[c][n2][:, P * e : P * (e + 1)],
+                       w5_w[:, g, 2 * P * n : 2 * P * (n + 1)], w5_plane[:, N * g + P * n : N * g + P * (n + 1)], FP4X4,
+                       x_codes[g][j0 // S][:, j0 % S : j0 % S + P], x_scales[:, g, j0 : j0 + P],
+                       g == 0 and e == 0, g == 1 and e == 3)
+
+        out_rows = out.rearrange("(n p) j -> p n j", p=P)
+
+        def as_f32(x_tile):
+            return x_tile[:].rearrange("p j t -> p (j t)").bitcast(F32)
+
+        def finish(c):
+            quantize_x(1, x1, CH * c, CH * (c + 1))
+            final_passes(1, c)
+            for n2 in range(2):
+                res = row_tile()
+                (nc.vector.tensor_copy if n2 == 0 else nc.scalar.copy)(out=res[:], in_=acc[c][n2][:])
+                nc.sync.dma_start(
+                    out=out_rows[:, 2 * n2 : 2 * n2 + 2, CH * c : CH * (c + 1)],
+                    in_=res[:].rearrange("p (n j) -> p n j", n=2),
+                )
+
+        for u in range(2):
+            for c in (2 * u, 2 * u + 1):
+                final_passes(0, c)
+        for c in range(4):
+            pick(1, 3, x1, CH * c, CH * (c + 1), as_f32(x0[0])[:, CH * c : CH * (c + 1)])
+        for c in range(4):
+            finish(c)

@@ -52,11 +52,11 @@ def tile_list_gem_tray_scores_kernel(
             nc.vector.memset(t[:].bitcast(I32), 0)
             return t
 
-        def load_planes_side_by_side(queue, plane, src, quadrants=(0, 2, 1, 3)):
-            for q in quadrants:
+        def load_planes_side_by_side(queue, plane, src):
+            for r in range(4):
                 queue.dma_start(
-                    out=plane[32 * q : 32 * q + 4, :].bitcast(I32).rearrange("r (a c) -> r a c", a=2),
-                    in_=src[:, 4 * q : 4 * q + 4, :].bitcast(I32).rearrange("a r c -> r a c"),
+                    out=plane[r:P:32, :].bitcast(I32).rearrange("q (a c) -> q a c", a=2),
+                    in_=src[:, r:16:4, :].bitcast(I32).rearrange("a q c -> q a c"),
                 )
 
         def load_words(src, a):
@@ -69,21 +69,40 @@ def tile_list_gem_tray_scores_kernel(
             nc.vector.tensor_copy(t[:], src.indirect(idx[:]))
             return t
 
-        def load_weight(w, a, g):
-            t = big.tile([P, PACK, KP], F32, name="big", align_bytes=64)
+        def load_weight(w, a, g, t=None):
+            if t is None:
+                t = big.tile([P, PACK, KP], F32, name="big", align_bytes=64)
             nc.sync.dma_start(
                 out=t[:],
                 in_=w[KP * a : KP * (a + 1), KP * g : KP * (g + 1)].rearrange("(p i) c -> p i c", i=PACK),
             )
             return t
 
-        def round_weight(copy, raw, t=None):
-            if t is None:
-                t = half.tile([P, PACK * KP], BF16, name="half", align_bytes=64)
+        def load_weight_halves(w, a, g):
+            t = big.tile([P, 2, PACK, KP // 2], F32, name="big", align_bytes=64)
+            for u in range(2):
+                c0 = KP * g + KP // 2 * u
+                nc.sync.dma_start(
+                    out=t[:, u],
+                    in_=w[KP * a : KP * (a + 1), c0 : c0 + KP // 2].rearrange("(p i) c -> p i c", i=PACK),
+                )
+            return t
+
+        def round_weight(copy, raw):
+            t = half.tile([P, PACK * KP], BF16, name="half", align_bytes=64)
             copy(
                 out=t[:].rearrange("p (t m i) -> p m t i", t=PACK, i=PACK),
                 in_=raw[:].rearrange("p i (m t) -> p m t i", t=PACK),
             )
+            return t
+
+        def round_weight_halves(raw):
+            t = half.tile([P, PACK * KP], BF16, name="half", align_bytes=64)
+            for u in range(2):
+                nc.scalar.copy(
+                    out=t[:].rearrange("p (t m i) -> p m t i", t=PACK, i=PACK)[:, P // 2 * u : P // 2 * (u + 1)],
+                    in_=raw[:, u].rearrange("p i (m t) -> p m t i", t=PACK),
+                )
             return t
 
         def quantize(src, width, name):
@@ -202,19 +221,18 @@ def tile_list_gem_tray_scores_kernel(
         w4_raw01 = load_weight(w4, 0, 1)
         pages[0, 2] = load_page(0, 2)
         w4_raw11 = load_weight(w4, 1, 1)
-        pages[0, 3] = load_page(0, 3)
         w2_w = keep.tile([P, 2, 2 * M], U8, name="w2_w", align_bytes=64)
         nc.sync.dma_start(out=w2_w[:].bitcast(I32), in_=w2_words.bitcast(I32).rearrange("a p c -> p a c"))
         tab_w0 = load_words(tab_words, 0)
-        pages[1, 0] = load_page(1, 0)
+        pages[0, 3] = load_page(0, 3)
         tab_w1 = load_words(tab_words, 1)
+        pages[1, 0] = load_page(1, 0)
         w1_raw0 = load_weight(w1, 0, 0)
         pages[1, 1] = load_page(1, 1)
         pages[1, 2] = load_page(1, 2)
-        w1_raw1 = load_weight(w1, 1, 0)
+        w1_raw1 = load_weight_halves(w1, 1, 0)
         w3_raw0 = load_weight(w3, 0, 0)
         pages[1, 3] = load_page(1, 3)
-        w3_raw1 = load_weight(w3, 0, 1)
         w5_w = keep.tile([P, 2, 2 * N], U8, name="w5_w", align_bytes=64)
         nc.sync.dma_start(out=w5_w[:].bitcast(I32), in_=w5_words.bitcast(I32).rearrange("a p c -> p a c"))
 
@@ -223,25 +241,27 @@ def tile_list_gem_tray_scores_kernel(
         gain1 = deal_gain(wg1_nat, "gain1_")
         for a, raw in enumerate((w4_raw01, w4_raw11)):
             w4q[a, 1] = quantize(round_weight(nc.scalar.copy, raw)[:], KP, "w4_%d1" % a)
-        h2_late = [h2_rows(1, t) for t in range(PACK - 1)]
-        h2_last = h2_sums(1, PACK - 1)
+        h2_late = [h2_rows(1, t) for t in range(2)]
+        h2_held = {t: h2_sums(1, t) for t in (2, 3)}
 
-        def scatter_last_half(u, spent):
+        def scatter_half(t, u, spent):
             cols = slice(S // 2 * u, S // 2 * (u + 1))
-            nc.scalar.activation(out=spent[:, cols], in_=h2_last[:, cols], func=ACT.Abs)
+            nc.scalar.activation(out=spent, in_=h2_held[t][:, cols], func=ACT.Abs)
             nc.vector.tensor_tensor(
-                pages[1, 3][:].indirect(idx4[:, 16 * u : 16 * (u + 1)]), spent[:, cols], gain2[3][:, cols], ALU.mult
+                pages[1, t][:].indirect(idx4[:, 16 * u : 16 * (u + 1)]), spent, gain2[t][:, cols], ALU.mult
             )
 
         scatter(pages[1, 0], idx4, h2_late[0], gain2[0])
 
         v = []
         w1q = []
-        for a, (words, raw) in enumerate(((tab_w0, w1_raw0), (tab_w1, w1_raw1))):
+        for a, words in enumerate((tab_w0, tab_w1)):
             v.append(gather(words[:], idx1, U32, "v_%d" % a))
-            w1q.append(quantize(round_weight(nc.scalar.copy, raw)[:], KP, "w1_%d" % a))
+        w1q.append(quantize(round_weight(nc.scalar.copy, w1_raw0)[:], KP, "w1_0"))
+        w1q.append(quantize(round_weight_halves(w1_raw1)[:], KP, "w1_1"))
         scatter(pages[1, 1], idx4, h2_late[1], gain2[1])
-        scatter(pages[1, 2], idx4, h2_late[2], gain2[2])
+        scatter_half(2, 0, row_tile()[:, 0 : S // 2])
+        scatter_half(2, 1, w1_raw1[:, 1, 0, :])
 
         f_half = half.tile([P, S, PACK], BF16, name="half", align_bytes=64)
         b_rows = []
@@ -256,26 +276,35 @@ def tile_list_gem_tray_scores_kernel(
                 out=b_sb[:].rearrange("j (t p) -> j t p", t=PACK), in_=bb[:].rearrange("j (p t) -> j t p", t=PACK)
             )
             b_rows.append(b_sb)
-        for c in range(PACK):
-            ba = bank()
-            cols = slice(P * c, P * (c + 1))
-            for a in range(2):
-                codes, scales = w1q[a]
-                mx(ba[:], v[a][:, cols], v_scales[a][:, cols], FP8X4, codes[:], scales[:], a == 0, a == 1)
-            prod = row_tile()
-            nc.vector.tensor_tensor(prod[:], ba[:], b_rows[c][:], ALU.mult)
-            fb = bank()
-            for u, term in enumerate((prod, neg_ref)):
-                for t in range(PACK):
-                    nc.tensor.matmul(
-                        fb[:, P * t : P * (t + 1)], term[:, P * t : P * (t + 1)], ident[:],
-                        start=(u == 0 and t == 0), stop=(u == 1 and t == PACK - 1), is_transpose=True,
-                    )
-            nc.scalar.copy(out=f_half[:, cols, :], in_=fb[:].rearrange("p (t j) -> p j t", t=PACK))
-        scatter_last_half(0, b_rows[0])
+        w3_landing = big.tile([P, PACK, KP], F32, name="big", align_bytes=64)
+        prods = [w3_landing[:, c, :] for c in range(PACK - 1)] + [row_tile()[:]]
+        a_sums = [bank() for c in range(PACK)]
+        for a in range(2):
+            codes, scales = w1q[a]
+            for c in range(PACK):
+                cols = slice(P * c, P * (c + 1))
+                mx(a_sums[c][:], v[a][:, cols], v_scales[a][:, cols], FP8X4, codes[:], scales[:], a == 0, a == 1)
         w3q = [quantize(round_weight(nc.scalar.copy, w3_raw0)[:], KP, "w3_0")]
+        def add_turned(acc, term, first):
+            for t in range(PACK):
+                nc.tensor.matmul(
+                    acc[:, P * t : P * (t + 1)], term[:, P * t : P * (t + 1)], ident[:],
+                    start=(first and t == 0), stop=(not first and t == PACK - 1), is_transpose=True,
+                )
+
+        f_sums = [bank() for c in range(PACK)]
+        for c in range(PACK):
+            nc.vector.tensor_tensor(prods[c], a_sums[c][:], b_rows[c][:], ALU.mult)
+            add_turned(f_sums[c], neg_ref, True)
+        for c in range(PACK):
+            add_turned(f_sums[c], prods[c], False)
+            nc.scalar.copy(
+                out=f_half[:, P * c : P * (c + 1), :], in_=f_sums[c][:].rearrange("p (t j) -> p j t", t=PACK)
+            )
+        scatter_half(3, 0, b_rows[0][:, 0 : S // 2])
         f_codes, f_scales = quantize(f_half[:].rearrange("p j t -> p (j t)"), S, "f")
-        scatter_last_half(1, neg_ref)
+        scatter_half(3, 1, prods[3][:, S // 2 : S])
+        w3_raw1 = load_weight(w3, 0, 1, w3_landing)
 
         x_codes = [[keep.tile([P, S], U32, name="x_codes%d%d" % (g, u), align_bytes=64) for u in range(2)] for g in range(2)]
         x_scales = keep.tile([P, 2, NPICK], U8, name="x_scales", align_bytes=64)
@@ -302,6 +331,7 @@ def tile_list_gem_tray_scores_kernel(
         def pick_all(g, t, x_half):
             picked = big.tile([P, NPICK], F32, name="big", align_bytes=64)
             pick(g, t, x_half, 0, NPICK, picked[:])
+            return picked
 
         def quantize_x(g, x_half, j0, j1):
             cols = slice(j0 % S, j0 % S + j1 - j0)
@@ -309,36 +339,20 @@ def tile_list_gem_tray_scores_kernel(
             nc.vector.quantize_mx(out=x_codes[g][j0 // S][:, cols].bitcast(FP8X4), scales=x_scales[:, g, j0:j1], in_=src)
 
         x0 = [half.tile([P, S, PACK], BF16, name="half", align_bytes=64) for u in range(2)]
-        w3_late = half.tile([P, PACK * KP], BF16, name="half", align_bytes=64)
         x1 = [half.tile([P, S, PACK], BF16, name="half", align_bytes=64) for u in range(2)]
         order = [(g, t) for g in range(2) for t in range(PACK)]
-        h1_other = keep.tile([P, S], F32, name="h1_other")
-        h = {0: h1_rows(0, 0, w3_late[:].bitcast(F32)[:, 0:S]), 1: h1_rows(0, 1, h1_other[:])}
-
-        def put(i):
-            g, t = order[i]
-            scatter(pages[g, t], idx3, h[i], gain1[t])
-
-        def fetch(i):
-            g, t = order[i]
-            pick_all(g, t, (x0, x1)[g])
-
-        for i in (0, 2, 4):
-            put(i)
-            h[i + 2] = h1_rows(*order[i + 2], h1_sb[:])
-            put(i + 1)
-            if i < 4:
-                h[i + 3] = h1_rows(*order[i + 3], h1_other[:])
+        h = h1_rows(0, 0, h1_sb[:])
+        spent = h1_sb[:]
+        for i, (g, t) in enumerate(order[:-1]):
+            scatter(pages[g, t], idx3, h, gain1[t])
+            h = h1_rows(*order[i + 1], spent)
             if i == 0:
-                w3q.append(quantize(round_weight(nc.scalar.copy, w3_raw1, w3_late)[:], KP, "w3_1"))
-            fetch(i)
-            fetch(i + 1)
-        put(6)
-        h[7] = h1_rows(*order[7], h1_sb[:])
-        quantize_x(0, x0, 0, S)
-        fetch(6)
-        put(7)
-        quantize_x(0, x0, S, 2 * S)
+                w3q.append(quantize(round_weight(nc.scalar.copy, w3_raw1)[:], KP, "w3_1"))
+            spent = pick_all(g, t, (x0, x1)[g])[:, 0:S]
+            if i == PACK:
+                for u in range(2):
+                    quantize_x(0, x0, S * u, S * (u + 1))
+        scatter(pages[1, 3], idx3, h, gain1[3])
 
         CH = 256
         acc = [[bank() for n2 in range(2)] for c in range(4)]

@@ -32,8 +32,9 @@ def tile_list_gem_tray_scores_kernel(
         lists = ctx.enter_context(tc.tile_pool(name="lists", bufs=1))
         keep = ctx.enter_context(tc.tile_pool(name="keep", bufs=1))
         big = ctx.enter_context(tc.tile_pool(name="big", bufs=6))
-        rows = ctx.enter_context(tc.tile_pool(name="rows", bufs=10))
+        rows = ctx.enter_context(tc.tile_pool(name="rows", bufs=9))
         half = ctx.enter_context(tc.tile_pool(name="half", bufs=4))
+        pair = ctx.enter_context(tc.tile_pool(name="pair", bufs=2))
         psum = ctx.enter_context(tc.psum_pool(name="psum", bufs=8))
 
         def bank():
@@ -64,8 +65,8 @@ def tile_list_gem_tray_scores_kernel(
             nc.sync.dma_start(out=t[:].bitcast(I32), in_=src[a].rearrange("p n i -> p (n i)").bitcast(I32))
             return t
 
-        def gather(src, idx, dtype, name):
-            t = keep.tile([P, S], dtype, name=name, align_bytes=64)
+        def gather(src, idx, dtype, name, pool=keep):
+            t = pool.tile([P, S], dtype, name=name, align_bytes=64)
             nc.vector.tensor_copy(t[:], src.indirect(idx[:]))
             return t
 
@@ -96,42 +97,47 @@ def tile_list_gem_tray_scores_kernel(
             )
             return t
 
-        def round_weight_halves(raw):
+        def round_weight_halves(copies, raw):
             t = half.tile([P, PACK * KP], BF16, name="half", align_bytes=64)
-            for u in range(2):
-                nc.scalar.copy(
+            for u, copy in enumerate(copies):
+                copy(
                     out=t[:].rearrange("p (t m i) -> p m t i", t=PACK, i=PACK)[:, P // 2 * u : P // 2 * (u + 1)],
                     in_=raw[:, u].rearrange("p i (m t) -> p m t i", t=PACK),
                 )
             return t
 
-        def quantize(src, width, name):
-            codes = keep.tile([P, width], U32, name=name + "_codes", align_bytes=64)
+        def quantize(src, width, name, pool=keep):
+            codes = pool.tile([P, width], U32, name=name + "_codes", align_bytes=64)
             scales = keep.tile([P, width], U8, name=name + "_scales", align_bytes=64)
             nc.vector.quantize_mx(out=codes[:].bitcast(FP8X4), scales=scales[:], in_=src)
             return codes, scales
 
-        def load_page(g, t):
-            pg = keep.tile([P, T2], F32, name="page%d_%d" % (g, t))
+        def load_page(i):
+            g, t = divmod(i, PACK)
+            pg = keep.tile([P, T2], F32, name="page%d" % i)
             nc.sync.dma_start(
                 out=pg[:], in_=page0[KP * g : KP * (g + 1), :].rearrange("(p t) c -> t p c", t=PACK)[t]
             )
             return pg
 
-        def load_gain(wg):
-            t = row_tile()
+        def load_gain(wg, name):
+            t = keep.tile([P, S], F32, name=name)
             nc.sync.dma_start(out=t[:], in_=wg)
             return t
 
-        def deal_gain(natural, name):
+        def turn_gain(natural):
+            banks = [bank() for c in range(PACK)]
+            for c in range(PACK):
+                for q in range(4):
+                    nc.tensor.transpose(banks[c][:, P * q : P * (q + 1)], natural[:, P * c : P * (c + 1)], ident[:])
+            return banks
+
+        def deal_gain(banks, name):
             turned = keep.tile([P, PACK, BANK], F32, name="turned")
             for c in range(PACK):
-                b = bank()
-                for q in range(4):
-                    nc.tensor.transpose(b[:, P * q : P * (q + 1)], natural[:, P * c : P * (c + 1)], ident[:])
                 nc.scalar.copy(
                     out=turned[:, c, :].rearrange("j (t p) -> j t p", t=PACK),
-                    in_=b[:].rearrange("j (p t) -> j t p", t=PACK),
+                    in_=banks[c][:].rearrange("j (p t) -> j t p", t=PACK),
                 )
             dealt = []
             for t in range(PACK):
@@ -152,139 +158,95 @@ def tile_list_gem_tray_scores_kernel(
         def scatter(pg, idx, h, gain):
             nc.vector.tensor_tensor(pg[:].indirect(idx[:]), h, gain[:], ALU.mult)
 
+        def load_fp4_words(src, name):
+            t = keep.tile([P, 2, src.shape[2]], U8, name=name, align_bytes=64)
+            nc.sync.dma_start(out=t[:].bitcast(I32), in_=src.bitcast(I32).rearrange("a p c -> p a c"))
+            return t
+
         ident = keep.tile([P, P], F32, name="ident")
         make_identity(nc, ident[:])
-        tab2_plane = zeroed_plane([P, T], "tab2_plane")
         tab_plane = zeroed_plane([P, 2 * T], "tab_plane")
         w2_plane = zeroed_plane([P, 2 * M], "w2_plane")
+        tab2_plane = zeroed_plane([P, T], "tab2_plane")
         w5_plane = zeroed_plane([P, 2 * N], "w5_plane")
 
-        def load_packed_planes(quadrants):
-            for q in quadrants:
-                nc.sync.dma_start(
-                    out=tab2_plane[32 * q : 32 * q + 8, :].bitcast(I32),
-                    in_=tab2_scales[:, 4 * q : 4 * q + 4, :].bitcast(I32),
-                )
-
-        wg2_nat = load_gain(wg2)
-        idx2 = load_list(offs2, "idx2")
+        wg1_nat = load_gain(wg1, "wg1_nat")
+        w2_w = load_fp4_words(w2_words, "w2_w")
         idx1 = load_list(offs, "idx1")
-        idx4 = load_list(offs4, "idx4")
         idx3 = load_list(offs3, "idx3")
+        idx2 = load_list(offs2, "idx2")
+        idx4 = load_list(offs4, "idx4")
         idx5 = load_list(offs5, "idx5")
-        tab2_w0 = load_words(tab2_words, 0)
-        load_packed_planes((0, 2, 1, 3))
-        w4_raw00 = load_weight(w4, 0, 0)
+        tab_w0 = load_words(tab_words, 0)
         load_planes_side_by_side(nc.sync, tab_plane, tab_scales)
-        w4_raw10 = load_weight(w4, 1, 0)
-        tab2_w1 = load_words(tab2_words, 1)
-        pages = {}
-        pages[0, 0] = load_page(0, 0)
+        w1_raw0 = load_weight(w1, 0, 0)
+        load_planes_side_by_side(nc.sync, w2_plane, w2_scales)
+        tab_w1 = load_words(tab_words, 1)
+        w1_raw1 = load_weight_halves(w1, 1, 0)
+        pages, w3_raw, w4_raw, tab2_w = {}, {}, {}, {}
+        pages[0] = load_page(0)
+        w3_raw[0] = load_weight(w3, 0, 0)
+        for q in range(4):
+            nc.sync.dma_start(
+                out=tab2_plane[32 * q : 32 * q + 8, :].bitcast(I32),
+                in_=tab2_scales[:, 4 * q : 4 * q + 4, :].bitcast(I32),
+            )
+        wg2_nat = load_gain(wg2, "wg2_nat")
+        tab2_w[0] = load_words(tab2_words, 0)
+        pages[1] = load_page(1)
+        w4_raw[0, 0] = load_weight(w4, 0, 0)
+        tab2_w[1] = load_words(tab2_words, 1)
+        pages[2] = load_page(2)
+        w4_raw[1, 0] = load_weight(w4, 1, 0)
+        pages[3] = load_page(3)
+        w3_raw[1] = load_weight(w3, 0, 1)
+        pages[4] = load_page(4)
+        w4_raw[0, 1] = load_weight(w4, 0, 1)
+        w4_raw[1, 1] = load_weight(w4, 1, 1)
+        pages[5] = load_page(5)
+        pages[6] = load_page(6)
+        pages[7] = load_page(7)
+        w5_w = load_fp4_words(w5_words, "w5_w")
 
         ref_col = keep.tile([P, PACK], F32, name="ref_col")
         nc.gpsimd.dma_start(out=ref_col[:], in_=ref.rearrange("(p t) -> p t", t=PACK))
-        load_planes_side_by_side(nc.gpsimd, w2_plane, w2_scales)
         vec_col = keep.tile([P, 2, PACK], F32, name="vec_col")
         nc.gpsimd.dma_start(out=vec_col[:], in_=vec.rearrange("(g p t) -> p g t", g=2, t=PACK))
         load_planes_side_by_side(nc.gpsimd, w5_plane, w5_scales)
 
-        gain2 = deal_gain(wg2_nat, "gain2_")
-        v2 = [gather(tab2_w0[:], idx2, U32, "v2_0")]
-        v2_scales = gather(tab2_plane[:], idx2, U8, "v2_scales")
-        w4q = {}
-        w4q[0, 0] = quantize(round_weight(nc.vector.tensor_copy, w4_raw00)[:], KP, "w4_00")
-        v_scales = [gather(tab_plane[:, T * a : T * (a + 1)], idx1, U8, "v_scales%d" % a) for a in range(2)]
-        w4q[1, 0] = quantize(round_weight(nc.scalar.copy, w4_raw10)[:], KP, "w4_10")
-        v2.append(gather(tab2_w1[:], idx2, U32, "v2_1"))
-
+        gain1 = deal_gain(turn_gain(wg1_nat), "gain1_")
         ref_bank = bank()
         for t in range(PACK):
             nc.tensor.transpose(ref_bank[:, P * t : P * (t + 1)], ref_col[:, t : t + 1].to_broadcast([P, P]), ident[:])
         neg_ref = keep.tile([P, M], F32, name="neg_ref")
         nc.scalar.activation(out=neg_ref[:], in_=ref_bank[:], func=ACT.Identity, scale=-1.0)
 
-        def h2_sums(g, t):
-            b = bank()
-            cols = slice(P * t, P * (t + 1))
-            for a in range(2):
-                codes, scales = w4q[a, g]
-                mx(b[:], codes[:, cols], scales[:, cols], FP8X4, v2[a][:], v2_scales[4 * a : P, :], a == 0, a == 1)
-            return b
+        v = [gather(tab_w0[:], idx1, U32, "v_0")]
+        v_scales = [gather(tab_plane[:, T * a : T * (a + 1)], idx1, U8, "v_scales%d" % a) for a in range(2)]
+        v.append(gather(tab_w1[:], idx1, U32, "v_1"))
+        w1q = [quantize(round_weight(nc.vector.tensor_copy, w1_raw0)[:], KP, "w1_0")]
+        w1q.append(quantize(round_weight_halves((nc.scalar.copy, nc.vector.tensor_copy), w1_raw1)[:], KP, "w1_1"))
 
-        def h2_rows(g, t):
-            h = row_tile()
-            nc.scalar.activation(out=h[:], in_=h2_sums(g, t)[:], func=ACT.Abs)
-            return h[:]
-
-        wg1_nat = load_gain(wg1)
-        pages[0, 1] = load_page(0, 1)
-        w4_raw01 = load_weight(w4, 0, 1)
-        pages[0, 2] = load_page(0, 2)
-        w4_raw11 = load_weight(w4, 1, 1)
-        w2_w = keep.tile([P, 2, 2 * M], U8, name="w2_w", align_bytes=64)
-        nc.sync.dma_start(out=w2_w[:].bitcast(I32), in_=w2_words.bitcast(I32).rearrange("a p c -> p a c"))
-        tab_w0 = load_words(tab_words, 0)
-        pages[0, 3] = load_page(0, 3)
-        tab_w1 = load_words(tab_words, 1)
-        pages[1, 0] = load_page(1, 0)
-        w1_raw0 = load_weight(w1, 0, 0)
-        pages[1, 1] = load_page(1, 1)
-        pages[1, 2] = load_page(1, 2)
-        w1_raw1 = load_weight_halves(w1, 1, 0)
-        w3_raw0 = load_weight(w3, 0, 0)
-        pages[1, 3] = load_page(1, 3)
-        w5_w = keep.tile([P, 2, 2 * N], U8, name="w5_w", align_bytes=64)
-        nc.sync.dma_start(out=w5_w[:].bitcast(I32), in_=w5_words.bitcast(I32).rearrange("a p c -> p a c"))
-
-        for t in range(PACK):
-            scatter(pages[0, t], idx4, h2_rows(0, t), gain2[t])
-        gain1 = deal_gain(wg1_nat, "gain1_")
-        for a, raw in enumerate((w4_raw01, w4_raw11)):
-            w4q[a, 1] = quantize(round_weight(nc.scalar.copy, raw)[:], KP, "w4_%d1" % a)
-        h2_late = [h2_rows(1, t) for t in range(2)]
-        h2_held = {t: h2_sums(1, t) for t in (2, 3)}
-
-        def scatter_half(t, u, spent):
-            cols = slice(S // 2 * u, S // 2 * (u + 1))
-            nc.scalar.activation(out=spent, in_=h2_held[t][:, cols], func=ACT.Abs)
-            nc.vector.tensor_tensor(
-                pages[1, t][:].indirect(idx4[:, 16 * u : 16 * (u + 1)]), spent, gain2[t][:, cols], ALU.mult
-            )
-
-        scatter(pages[1, 0], idx4, h2_late[0], gain2[0])
-
-        v = []
-        w1q = []
-        for a, words in enumerate((tab_w0, tab_w1)):
-            v.append(gather(words[:], idx1, U32, "v_%d" % a))
-        w1q.append(quantize(round_weight(nc.scalar.copy, w1_raw0)[:], KP, "w1_0"))
-        w1q.append(quantize(round_weight_halves(w1_raw1)[:], KP, "w1_1"))
-        scatter(pages[1, 1], idx4, h2_late[1], gain2[1])
-        scatter_half(2, 0, row_tile()[:, 0 : S // 2])
-        scatter_half(2, 1, w1_raw1[:, 1, 0, :])
-
-        f_half = half.tile([P, S, PACK], BF16, name="half", align_bytes=64)
+        b_sums = [bank() for c in range(PACK)]
+        for a in range(2):
+            for c in range(PACK):
+                cols = slice(P * c, P * (c + 1))
+                mx(b_sums[c][:], v[a][:, cols], v_scales[a][:, cols], FP8X4,
+                   w2_w[:, a, :], w2_plane[:, M * a : M * (a + 1)], a == 0, a == 1, FP4X4)
         b_rows = []
         for c in range(PACK):
-            bb = bank()
-            cols = slice(P * c, P * (c + 1))
-            for a in range(2):
-                mx(bb[:], v[a][:, cols], v_scales[a][:, cols], FP8X4,
-                   w2_w[:, a, :], w2_plane[:, M * a : M * (a + 1)], a == 0, a == 1, FP4X4)
             b_sb = row_tile()
             nc.scalar.copy(
-                out=b_sb[:].rearrange("j (t p) -> j t p", t=PACK), in_=bb[:].rearrange("j (p t) -> j t p", t=PACK)
+                out=b_sb[:].rearrange("j (t p) -> j t p", t=PACK), in_=b_sums[c][:].rearrange("j (p t) -> j t p", t=PACK)
             )
             b_rows.append(b_sb)
-        w3_landing = big.tile([P, PACK, KP], F32, name="big", align_bytes=64)
-        prods = [w3_landing[:, c, :] for c in range(PACK - 1)] + [row_tile()[:]]
         a_sums = [bank() for c in range(PACK)]
         for a in range(2):
             codes, scales = w1q[a]
             for c in range(PACK):
                 cols = slice(P * c, P * (c + 1))
                 mx(a_sums[c][:], v[a][:, cols], v_scales[a][:, cols], FP8X4, codes[:], scales[:], a == 0, a == 1)
-        w3q = [quantize(round_weight(nc.scalar.copy, w3_raw0)[:], KP, "w3_0")]
+
         def add_turned(acc, term, first):
             for t in range(PACK):
                 nc.tensor.matmul(
@@ -293,45 +255,78 @@ def tile_list_gem_tray_scores_kernel(
                 )
 
         f_sums = [bank() for c in range(PACK)]
+        prods = []
         for c in range(PACK):
-            nc.vector.tensor_tensor(prods[c], a_sums[c][:], b_rows[c][:], ALU.mult)
-            add_turned(f_sums[c], neg_ref, True)
+            prods.append(row_tile())
+            nc.vector.tensor_tensor(prods[c][:], a_sums[c][:], b_rows[c][:], ALU.mult)
+        w3q = [quantize(round_weight(nc.vector.tensor_copy, w3_raw[0])[:], KP, "w3_0")]
+        f_half = half.tile([P, S, PACK], BF16, name="half", align_bytes=64)
         for c in range(PACK):
-            add_turned(f_sums[c], prods[c], False)
+            add_turned(f_sums[c], prods[c], True)
+            add_turned(f_sums[c], neg_ref, False)
             nc.scalar.copy(
                 out=f_half[:, P * c : P * (c + 1), :], in_=f_sums[c][:].rearrange("p (t j) -> p j t", t=PACK)
             )
-        scatter_half(3, 0, b_rows[0][:, 0 : S // 2])
-        f_codes, f_scales = quantize(f_half[:].rearrange("p j t -> p (j t)"), S, "f")
-        scatter_half(3, 1, prods[3][:, S // 2 : S])
-        w3_raw1 = load_weight(w3, 0, 1, w3_landing)
+        f_codes, f_scales = quantize(f_half[:].rearrange("p j t -> p (j t)"), S, "f", pair)
 
-        x_codes = [[keep.tile([P, S], U32, name="x_codes%d%d" % (g, u), align_bytes=64) for u in range(2)] for g in range(2)]
-        x_scales = keep.tile([P, 2, NPICK], U8, name="x_scales", align_bytes=64)
-
-        def h1_rows(g, t, h):
+        def h1_sums(i):
+            g, t = divmod(i, PACK)
             b = bank()
             cols = slice(P * t, P * (t + 1))
             codes, scales = w3q[g]
             mx(b[:], codes[:, cols], scales[:, cols], FP8X4, f_codes[:], f_scales[:], True, True)
-            nc.scalar.copy(out=h, in_=b[:])
+            return b
+
+        def h1_rows(i, h):
+            nc.scalar.copy(out=h, in_=h1_sums(i)[:])
             return h
 
-        h1_sb = keep.tile([P, S], F32, name="h1_sb")
+        def h2_rows(i, h):
+            g, t = divmod(i, PACK)
+            b = bank()
+            cols = slice(P * t, P * (t + 1))
+            for a in range(2):
+                codes, scales = w4q[a, g]
+                mx(b[:], codes[:, cols], scales[:, cols], FP8X4, v2[a][:], v2_scales[4 * a : P, :], a == 0, a == 1)
+            nc.scalar.activation(out=h, in_=b[:], func=ACT.Abs)
+            return h
 
-        def pick(g, t, x_half, j0, j1, picked):
-            nc.vector.tensor_copy(picked, pages[g, t][:].indirect(idx5[:, j0 // 16 : j1 // 16]))
+        w4q = {}
+
+        def quantize_w4(a, g):
+            w4q[a, g] = quantize(round_weight(nc.scalar.copy, w4_raw[a, g])[:], KP, "w4_%d%d" % (a, g))
+
+        wg2_banks = turn_gain(wg2_nat)
+        h1 = [h1_rows(i, row_tile()[:]) for i in range(PACK - 1)]
+        h1_held = h1_sums(PACK - 1)
+        v2 = [gather(tab2_w[0][:], idx2, U32, "f_codes", pair)]
+        scatter(pages[0], idx3, h1[0], gain1[0])
+        v2_scales = gather(tab2_plane[:], idx2, U8, "v2_scales")
+        v2.append(gather(tab2_w[1][:], idx2, U32, "v2_1"))
+        gain2 = deal_gain(wg2_banks, "gain2_")
+        for a in range(2):
+            quantize_w4(a, 0)
+        for i in range(1, PACK - 1):
+            scatter(pages[i], idx3, h1[i], gain1[i])
+        for u, h in enumerate((row_tile()[:, 0 : S // 2], w4_raw[1, 0][:, 0, 0 : S // 2])):
+            cols = slice(S // 2 * u, S // 2 * (u + 1))
+            nc.scalar.copy(out=h, in_=h1_held[:, cols])
+            nc.vector.tensor_tensor(
+                pages[3][:].indirect(idx3[:, 16 * u : 16 * (u + 1)]), h, gain1[3][:, cols], ALU.mult
+            )
+
+        x_codes = [[keep.tile([P, S], U32, name="x_codes%d%d" % (g, u), align_bytes=64) for u in range(2)] for g in range(2)]
+        x_scales = keep.tile([P, 2, NPICK], U8, name="x_scales", align_bytes=64)
+
+        def pick(i, x_half, j0, j1, picked):
+            g, t = divmod(i, PACK)
+            nc.vector.tensor_copy(picked, pages[i][:].indirect(idx5[:, j0 // 16 : j1 // 16]))
             for lo in range(j0, j1, S):
                 hi = min(lo + S, j1)
                 nc.scalar.activation(
                     out=x_half[lo // S][:, lo % S : lo % S + hi - lo, t], in_=picked[:, lo - j0 : hi - j0],
                     func=ACT.Identity, bias=vec_col[:, g, t : t + 1],
                 )
-
-        def pick_all(g, t, x_half):
-            picked = big.tile([P, NPICK], F32, name="big", align_bytes=64)
-            pick(g, t, x_half, 0, NPICK, picked[:])
-            return picked
 
         def quantize_x(g, x_half, j0, j1):
             cols = slice(j0 % S, j0 % S + j1 - j0)
@@ -340,19 +335,25 @@ def tile_list_gem_tray_scores_kernel(
 
         x0 = [half.tile([P, S, PACK], BF16, name="half", align_bytes=64) for u in range(2)]
         x1 = [half.tile([P, S, PACK], BF16, name="half", align_bytes=64) for u in range(2)]
-        order = [(g, t) for g in range(2) for t in range(PACK)]
-        h = h1_rows(0, 0, h1_sb[:])
-        spent = h1_sb[:]
-        for i, (g, t) in enumerate(order[:-1]):
-            scatter(pages[g, t], idx3, h, gain1[t])
-            h = h1_rows(*order[i + 1], spent)
+        h2_sb = keep.tile([P, S], F32, name="h2_sb")
+        h = h2_rows(0, h2_sb[:])
+        spent = None
+        for i in range(2 * PACK - 1):
+            scatter(pages[i], idx4, h, gain2[i % PACK])
+            h = h2_rows(i + 1, h2_sb[:] if i == 0 else spent[:, 0:S])
             if i == 0:
-                w3q.append(quantize(round_weight(nc.scalar.copy, w3_raw1)[:], KP, "w3_1"))
-            spent = pick_all(g, t, (x0, x1)[g])[:, 0:S]
+                w3q.append(quantize(round_weight(nc.scalar.copy, w3_raw[1])[:], KP, "w3_1"))
+            if i in (0, 1):
+                quantize_w4((0, 1).index(i), 1)
+            late = i + 2
+            if PACK <= late < 2 * PACK:
+                scatter(pages[late], idx3, h1_rows(late, spent[:, S:NPICK]), gain1[late % PACK])
+            spent = big.tile([P, NPICK], F32, name="big", align_bytes=64)
+            pick(i, (x0, x1)[i // PACK], 0, NPICK, spent[:])
             if i == PACK:
                 for u in range(2):
                     quantize_x(0, x0, S * u, S * (u + 1))
-        scatter(pages[1, 3], idx3, h, gain1[3])
+        scatter(pages[7], idx4, h, gain2[3])
 
         CH = 256
         acc = [[bank() for n2 in range(2)] for c in range(4)]
@@ -386,6 +387,6 @@ def tile_list_gem_tray_scores_kernel(
             for c in (2 * u, 2 * u + 1):
                 final_passes(0, c)
         for c in range(4):
-            pick(1, 3, x1, CH * c, CH * (c + 1), as_f32(x0[0])[:, CH * c : CH * (c + 1)])
+            pick(7, x1, CH * c, CH * (c + 1), as_f32(x0[0])[:, CH * c : CH * (c + 1)])
         for c in range(4):
             finish(c)

@@ -33,7 +33,7 @@ def tile_list_gem_tray_scores_kernel(
         keep = ctx.enter_context(tc.tile_pool(name="keep", bufs=1))
         big = ctx.enter_context(tc.tile_pool(name="big", bufs=6))
         rows = ctx.enter_context(tc.tile_pool(name="rows", bufs=9))
-        half = ctx.enter_context(tc.tile_pool(name="half", bufs=4))
+        half = ctx.enter_context(tc.tile_pool(name="half", bufs=5))
         pair = ctx.enter_context(tc.tile_pool(name="pair", bufs=2))
         psum = ctx.enter_context(tc.psum_pool(name="psum", bufs=8))
 
@@ -200,9 +200,9 @@ def tile_list_gem_tray_scores_kernel(
         w4_raw[1, 0] = load_weight(w4, 1, 0)
         pages[3] = load_page(3)
         w3_raw[1] = load_weight(w3, 0, 1)
-        pages[4] = load_page(4)
         w4_raw[0, 1] = load_weight(w4, 0, 1)
         w4_raw[1, 1] = load_weight(w4, 1, 1)
+        pages[4] = load_page(4)
         pages[5] = load_page(5)
         pages[6] = load_page(6)
         pages[7] = load_page(7)
@@ -308,14 +308,10 @@ def tile_list_gem_tray_scores_kernel(
             quantize_w4(a, 0)
         for i in range(1, PACK - 1):
             scatter(pages[i], idx3, h1[i], gain1[i])
-        for u, h in enumerate((row_tile()[:, 0 : S // 2], w4_raw[1, 0][:, 0, 0 : S // 2])):
-            cols = slice(S // 2 * u, S // 2 * (u + 1))
-            nc.scalar.copy(out=h, in_=h1_held[:, cols])
-            nc.vector.tensor_tensor(
-                pages[3][:].indirect(idx3[:, 16 * u : 16 * (u + 1)]), h, gain1[3][:, cols], ALU.mult
-            )
+        nc.scalar.copy(out=w4_raw[1, 0][:, 0, :], in_=h1_held[:])
+        scatter(pages[3], idx3, w4_raw[1, 0][:, 0, :], gain1[3])
 
-        x_codes = [[keep.tile([P, S], U32, name="x_codes%d%d" % (g, u), align_bytes=64) for u in range(2)] for g in range(2)]
+        x_codes = {(g, u): keep.tile([P, S], U32, name="x_codes%d%d" % (g, u), align_bytes=64) for g, u in ((0, 0), (1, 0), (1, 1))}
         x_scales = keep.tile([P, 2, NPICK], U8, name="x_scales", align_bytes=64)
 
         def pick(i, x_half, j0, j1, picked):
@@ -331,28 +327,26 @@ def tile_list_gem_tray_scores_kernel(
         def quantize_x(g, x_half, j0, j1):
             cols = slice(j0 % S, j0 % S + j1 - j0)
             src = x_half[j0 // S][:, cols, :].rearrange("p j t -> p (j t)")
-            nc.vector.quantize_mx(out=x_codes[g][j0 // S][:, cols].bitcast(FP8X4), scales=x_scales[:, g, j0:j1], in_=src)
+            nc.vector.quantize_mx(out=x_codes[g, j0 // S][:, cols].bitcast(FP8X4), scales=x_scales[:, g, j0:j1], in_=src)
 
         x0 = [half.tile([P, S, PACK], BF16, name="half", align_bytes=64) for u in range(2)]
         x1 = [half.tile([P, S, PACK], BF16, name="half", align_bytes=64) for u in range(2)]
-        h2_sb = keep.tile([P, S], F32, name="h2_sb")
-        h = h2_rows(0, h2_sb[:])
+        h = h2_rows(0, row_tile()[:])
         spent = None
         for i in range(2 * PACK - 1):
             scatter(pages[i], idx4, h, gain2[i % PACK])
-            h = h2_rows(i + 1, h2_sb[:] if i == 0 else spent[:, 0:S])
+            h = h2_rows(i + 1, row_tile()[:] if i < 2 else spent[:, 0:S])
             if i == 0:
                 w3q.append(quantize(round_weight(nc.scalar.copy, w3_raw[1])[:], KP, "w3_1"))
-            if i in (0, 1):
-                quantize_w4((0, 1).index(i), 1)
+                for a in range(2):
+                    quantize_w4(a, 1)
             late = i + 2
             if PACK <= late < 2 * PACK:
                 scatter(pages[late], idx3, h1_rows(late, spent[:, S:NPICK]), gain1[late % PACK])
             spent = big.tile([P, NPICK], F32, name="big", align_bytes=64)
             pick(i, (x0, x1)[i // PACK], 0, NPICK, spent[:])
             if i == PACK:
-                for u in range(2):
-                    quantize_x(0, x0, S * u, S * (u + 1))
+                quantize_x(0, x0, 0, S)
         scatter(pages[7], idx4, h, gain2[3])
 
         CH = 256
@@ -364,7 +358,7 @@ def tile_list_gem_tray_scores_kernel(
                     n, j0 = 2 * n2 + e // 2, CH * c + P * (e % 2)
                     mx(acc[c][n2][:, P * e : P * (e + 1)],
                        w5_w[:, g, 2 * P * n : 2 * P * (n + 1)], w5_plane[:, N * g + P * n : N * g + P * (n + 1)], FP4X4,
-                       x_codes[g][j0 // S][:, j0 % S : j0 % S + P], x_scales[:, g, j0 : j0 + P],
+                       x_codes[g, j0 // S][:, j0 % S : j0 % S + P], x_scales[:, g, j0 : j0 + P],
                        g == 0 and e == 0, g == 1 and e == 3)
 
         out_rows = out.rearrange("(n p) j -> p n j", p=P)
@@ -383,10 +377,19 @@ def tile_list_gem_tray_scores_kernel(
                     in_=res[:].rearrange("p (n j) -> p n j", n=2),
                 )
 
-        for u in range(2):
-            for c in (2 * u, 2 * u + 1):
-                final_passes(0, c)
+        for c in range(2):
+            final_passes(0, c)
         for c in range(4):
-            pick(7, x1, CH * c, CH * (c + 1), as_f32(x0[0])[:, CH * c : CH * (c + 1)])
-        for c in range(4):
+            if c == 1:
+                picked = pair.tile([P, CH], F32, name="last", align_bytes=64)[:]
+            else:
+                picked = as_f32(x0[0])[:, CH * c : CH * (c + 1)]
+            pick(7, x1, CH * c, CH * (c + 1), picked)
+            if c == 1:
+                x_codes[0, 1] = pair.tile([P, S], U32, name="last", align_bytes=64)
+                quantize_x(0, x0, S, 2 * S)
+        finish(0)
+        for c in range(2, 4):
+            final_passes(0, c)
+        for c in range(1, 4):
             finish(c)

from contextlib import ExitStack

import concourse.mybir as mybir
from concourse.masks import make_identity

K, T, S, M, H, T2, NPICK, N = 1024, 2048, 512, 512, 1024, 2048, 1024, 512
FLOPS = 2 * (2 * K * M * S + M * H * S + K * H * S + H * N * NPICK)

F32 = mybir.dt.float32
BF16 = mybir.dt.bfloat16
I32 = mybir.dt.int32
U32 = mybir.dt.uint32
U16 = mybir.dt.uint16
U8 = mybir.dt.uint8
FP8X4 = mybir.dt.float8_e4m3fn_x4
FP4X4 = mybir.dt.float4_e2m1fn_x4
ACT = mybir.ActivationFunctionType
ALU = mybir.AluOpType

P = 128
PACK = 4
KP = P * PACK
BANK = 512


def tile_list_gem_tray_scores_kernel(
    tc, tab_words, tab_scales, tab2_words, tab2_scales, offs, offs2, offs3, offs4, offs5,
    w1, w2_words, w2_scales, ref, w3, w4, page0, wg1, wg2, vec, w5_words, w5_scales, out,
):
    nc = tc.nc
    with ExitStack() as ctx:
        lists = ctx.enter_context(tc.tile_pool(name="lists", bufs=1))
        keep = ctx.enter_context(tc.tile_pool(name="keep", bufs=1))
        big = ctx.enter_context(tc.tile_pool(name="big", bufs=6))
        rows = ctx.enter_context(tc.tile_pool(name="rows", bufs=9))
        half = ctx.enter_context(tc.tile_pool(name="half", bufs=5))
        pair = ctx.enter_context(tc.tile_pool(name="pair", bufs=2))
        psum = ctx.enter_context(tc.psum_pool(name="psum", bufs=8))

        def bank():
            return psum.tile([P, BANK], F32, name="bank")

        def row_tile():
            return rows.tile([P, S], F32, name="row")

        def load_list(src, name):
            t = lists.tile([P, src.shape[1]], U16, name=name)
            nc.sync.dma_start(t[:], src)
            return t

        def zeroed_plane(shape, name):
            t = keep.tile(shape, U8, name=name, align_bytes=64)
            nc.vector.memset(t[:].bitcast(I32), 0)
            return t

        def load_planes_side_by_side(queue, plane, src):
            for r in range(4):
                queue.dma_start(
                    out=plane[r:P:32, :].bitcast(I32).rearrange("q (a c) -> q a c", a=2),
                    in_=src[:, r:16:4, :].bitcast(I32).rearrange("a q c -> q a c"),
                )

        def load_words(src, a):
            t = big.tile([P, T], U32, name="big", align_bytes=64)
            nc.sync.dma_start(out=t[:].bitcast(I32), in_=src[a].rearrange("p n i -> p (n i)").bitcast(I32))
            return t

        def gather(src, idx, dtype, name, pool=keep):
            t = pool.tile([P, S], dtype, name=name, align_bytes=64)
            nc.vector.tensor_copy(t[:], src.indirect(idx[:]))
            return t

        def load_weight(w, a, g, t=None):
            if t is None:
                t = big.tile([P, PACK, KP], F32, name="big", align_bytes=64)
            nc.sync.dma_start(
                out=t[:],
                in_=w[KP * a : KP * (a + 1), KP * g : KP * (g + 1)].rearrange("(p i) c -> p i c", i=PACK),
            )
            return t

        def load_weight_halves(w, a, g):
            t = big.tile([P, 2, PACK, KP // 2], F32, name="big", align_bytes=64)
            for u in range(2):
                c0 = KP * g + KP // 2 * u
                nc.sync.dma_start(
                    out=t[:, u],
                    in_=w[KP * a : KP * (a + 1), c0 : c0 + KP // 2].rearrange("(p i) c -> p i c", i=PACK),
                )
            return t

        def round_weight(copy, raw):
            t = half.tile([P, PACK * KP], BF16, name="half", align_bytes=64)
            copy(
                out=t[:].rearrange("p (t m i) -> p m t i", t=PACK, i=PACK),
                in_=raw[:].rearrange("p i (m t) -> p m t i", t=PACK),
            )
            return t

        def round_weight_halves(copies, raw):
            t = half.tile([P, PACK * KP], BF16, name="half", align_bytes=64)
            for u, copy in enumerate(copies):
                copy(
                    out=t[:].rearrange("p (t m i) -> p m t i", t=PACK, i=PACK)[:, P // 2 * u : P // 2 * (u + 1)],
                    in_=raw[:, u].rearrange("p i (m t) -> p m t i", t=PACK),
                )
            return t

        def quantize(src, width, name, pool=keep):
            codes = pool.tile([P, width], U32, name=name + "_codes", align_bytes=64)
            scales = keep.tile([P, width], U8, name=name + "_scales", align_bytes=64)
            nc.vector.quantize_mx(out=codes[:].bitcast(FP8X4), scales=scales[:], in_=src)
            return codes, scales

        def load_page(i):
            g, t = divmod(i, PACK)
            pg = keep.tile([P, T2], F32, name="page%d" % i)
            nc.sync.dma_start(
                out=pg[:], in_=page0[KP * g : KP * (g + 1), :].rearrange("(p t) c -> t p c", t=PACK)[t]
            )
            return pg

        def load_gain(wg, name):
            t = keep.tile([P, S], F32, name=name)
            nc.sync.dma_start(out=t[:], in_=wg)
            return t

        def turn_gain(natural):
            banks = [bank() for c in range(PACK)]
            for c in range(PACK):
                for q in range(4):
                    nc.tensor.transpose(banks[c][:, P * q : P * (q + 1)], natural[:, P * c : P * (c + 1)], ident[:])
            return banks

        def deal_gain(banks, name):
            turned = keep.tile([P, PACK, BANK], F32, name="turned")
            for c in range(PACK):
                nc.scalar.copy(
                    out=turned[:, c, :].rearrange("j (t p) -> j t p", t=PACK),
                    in_=banks[c][:].rearrange("j (p t) -> j t p", t=PACK),
                )
            dealt = []
            for t in range(PACK):
                b = bank()
                for c in range(PACK):
                    nc.tensor.transpose(b[:, P * c : P * (c + 1)], turned[:, c, P * t : P * (t + 1)], ident[:])
                d = keep.tile([P, S], F32, name="%s%d" % (name, t))
                nc.scalar.copy(out=d[:], in_=b[:])
                dealt.append(d)
            return dealt

        def mx(acc, lhs, lhs_scale, lhs_dtype, rhs, rhs_scale, start, stop, rhs_dtype=FP8X4):
            nc.tensor.matmul_mx(
                out=acc, lhsT=lhs.bitcast(lhs_dtype), lhsT_scale=lhs_scale,
                rhs=rhs.bitcast(rhs_dtype), rhs_scale=rhs_scale, start=start, stop=stop,
            )

        def scatter(pg, idx, h, gain):
            nc.vector.tensor_tensor(pg[:].indirect(idx[:]), h, gain[:], ALU.mult)

        def load_fp4_words(src, name):
            t = keep.tile([P, 2, src.shape[2]], U8, name=name, align_bytes=64)
            nc.sync.dma_start(out=t[:].bitcast(I32), in_=src.bitcast(I32).rearrange("a p c -> p a c"))
            return t

        ident = keep.tile([P, P], F32, name="ident")
        make_identity(nc, ident[:])
        tab_plane = zeroed_plane([P, 2 * T], "tab_plane")
        w2_plane = zeroed_plane([P, 2 * M], "w2_plane")
        tab2_plane = zeroed_plane([P, T], "tab2_plane")
        w5_plane = zeroed_plane([P, 2 * N], "w5_plane")

        wg1_nat = load_gain(wg1, "wg1_nat")
        w2_w = load_fp4_words(w2_words, "w2_w")
        idx1 = load_list(offs, "idx1")
        idx3 = load_list(offs3, "idx3")
        idx2 = load_list(offs2, "idx2")
        idx4 = load_list(offs4, "idx4")
        idx5 = load_list(offs5, "idx5")
        tab_w0 = load_words(tab_words, 0)
        load_planes_side_by_side(nc.sync, tab_plane, tab_scales)
        w1_raw0 = load_weight(w1, 0, 0)
        load_planes_side_by_side(nc.sync, w2_plane, w2_scales)
        tab_w1 = load_words(tab_words, 1)
        w1_raw1 = load_weight_halves(w1, 1, 0)
        pages, w3_raw, w4_raw, tab2_w = {}, {}, {}, {}
        pages[0] = load_page(0)
        w3_raw[0] = load_weight(w3, 0, 0)
        for q in range(4):
            nc.sync.dma_start(
                out=tab2_plane[32 * q : 32 * q + 8, :].bitcast(I32),
                in_=tab2_scales[:, 4 * q : 4 * q + 4, :].bitcast(I32),
            )
        wg2_nat = load_gain(wg2, "wg2_nat")
        tab2_w[0] = load_words(tab2_words, 0)
        pages[1] = load_page(1)
        w4_raw[0, 0] = load_weight(w4, 0, 0)
        tab2_w[1] = load_words(tab2_words, 1)
        pages[2] = load_page(2)
        w4_raw[1, 0] = load_weight(w4, 1, 0)
        pages[3] = load_page(3)
        w3_raw[1] = load_weight(w3, 0, 1)
        w4_raw[0, 1] = load_weight(w4, 0, 1)
        w4_raw[1, 1] = load_weight(w4, 1, 1)
        pages[4] = load_page(4)
        pages[5] = load_page(5)
        pages[6] = load_page(6)
        pages[7] = load_page(7)
        w5_w = load_fp4_words(w5_words, "w5_w")

        ref_col = keep.tile([P, PACK], F32, name="ref_col")
        nc.gpsimd.dma_start(out=ref_col[:], in_=ref.rearrange("(p t) -> p t", t=PACK))
        vec_col = keep.tile([P, 2, PACK], F32, name="vec_col")
        nc.gpsimd.dma_start(out=vec_col[:], in_=vec.rearrange("(g p t) -> p g t", g=2, t=PACK))
        load_planes_side_by_side(nc.gpsimd, w5_plane, w5_scales)

        gain1 = deal_gain(turn_gain(wg1_nat), "gain1_")
        ref_bank = bank()
        for t in range(PACK):
            nc.tensor.transpose(ref_bank[:, P * t : P * (t + 1)], ref_col[:, t : t + 1].to_broadcast([P, P]), ident[:])
        neg_ref = keep.tile([P, M], F32, name="neg_ref")
        nc.scalar.activation(out=neg_ref[:], in_=ref_bank[:], func=ACT.Identity, scale=-1.0)

        v = [gather(tab_w0[:], idx1, U32, "v_0")]
        v_scales = [gather(tab_plane[:, T * a : T * (a + 1)], idx1, U8, "v_scales%d" % a) for a in range(2)]
        v.append(gather(tab_w1[:], idx1, U32, "v_1"))
        w1q = [quantize(round_weight(nc.vector.tensor_copy, w1_raw0)[:], KP, "w1_0")]
        w1q.append(quantize(round_weight_halves((nc.scalar.copy, nc.vector.tensor_copy), w1_raw1)[:], KP, "w1_1"))

        b_sums = [bank() for c in range(PACK)]
        for a in range(2):
            for c in range(PACK):
                cols = slice(P * c, P * (c + 1))
                mx(b_sums[c][:], v[a][:, cols], v_scales[a][:, cols], FP8X4,
                   w2_w[:, a, :], w2_plane[:, M * a : M * (a + 1)], a == 0, a == 1, FP4X4)
        b_rows = []
        for c in range(PACK):
            b_sb = row_tile()
            nc.scalar.copy(
                out=b_sb[:].rearrange("j (t p) -> j t p", t=PACK), in_=b_sums[c][:].rearrange("j (p t) -> j t p", t=PACK)
            )
            b_rows.append(b_sb)
        a_sums = [bank() for c in range(PACK)]
        for a in range(2):
            codes, scales = w1q[a]
            for c in range(PACK):
                cols = slice(P * c, P * (c + 1))
                mx(a_sums[c][:], v[a][:, cols], v_scales[a][:, cols], FP8X4, codes[:], scales[:], a == 0, a == 1)

        def add_turned(acc, term, first):
            for t in range(PACK):
                nc.tensor.matmul(
                    acc[:, P * t : P * (t + 1)], term[:, P * t : P * (t + 1)], ident[:],
                    start=(first and t == 0), stop=(not first and t == PACK - 1), is_transpose=True,
                )

        f_sums = [bank() for c in range(PACK)]
        prods = []
        for c in range(PACK):
            prods.append(row_tile())
            nc.vector.tensor_tensor(prods[c][:], a_sums[c][:], b_rows[c][:], ALU.mult)
        w3q = [quantize(round_weight(nc.vector.tensor_copy, w3_raw[0])[:], KP, "w3_0")]
        f_half = half.tile([P, S, PACK], BF16, name="half", align_bytes=64)
        for c in range(PACK):
            add_turned(f_sums[c], prods[c], True)
            add_turned(f_sums[c], neg_ref, False)
            nc.scalar.copy(
                out=f_half[:, P * c : P * (c + 1), :], in_=f_sums[c][:].rearrange("p (t j) -> p j t", t=PACK)
            )
        f_codes, f_scales = quantize(f_half[:].rearrange("p j t -> p (j t)"), S, "f", pair)

        def h1_sums(i):
            g, t = divmod(i, PACK)
            b = bank()
            cols = slice(P * t, P * (t + 1))
            codes, scales = w3q[g]
            mx(b[:], codes[:, cols], scales[:, cols], FP8X4, f_codes[:], f_scales[:], True, True)
            return b

        def h1_rows(i, h):
            nc.scalar.copy(out=h, in_=h1_sums(i)[:])
            return h

        def h2_rows(i, h):
            g, t = divmod(i, PACK)
            b = bank()
            cols = slice(P * t, P * (t + 1))
            for a in range(2):
                codes, scales = w4q[a, g]
                mx(b[:], codes[:, cols], scales[:, cols], FP8X4, v2[a][:], v2_scales[4 * a : P, :], a == 0, a == 1)
            nc.scalar.activation(out=h, in_=b[:], func=ACT.Abs)
            return h

        w4q = {}

        def quantize_w4(a, g):
            w4q[a, g] = quantize(round_weight(nc.scalar.copy, w4_raw[a, g])[:], KP, "w4_%d%d" % (a, g))

        wg2_banks = turn_gain(wg2_nat)
        h1 = [h1_rows(i, row_tile()[:]) for i in range(PACK - 1)]
        h1_held = h1_sums(PACK - 1)
        v2 = [gather(tab2_w[0][:], idx2, U32, "f_codes", pair)]
        scatter(pages[0], idx3, h1[0], gain1[0])
        v2_scales = gather(tab2_plane[:], idx2, U8, "v2_scales")
        v2.append(gather(tab2_w[1][:], idx2, U32, "v2_1"))
        gain2 = deal_gain(wg2_banks, "gain2_")
        for a in range(2):
            quantize_w4(a, 0)
        for i in range(1, PACK - 1):
            scatter(pages[i], idx3, h1[i], gain1[i])
        nc.scalar.copy(out=w4_raw[1, 0][:, 0, :], in_=h1_held[:])
        scatter(pages[3], idx3, w4_raw[1, 0][:, 0, :], gain1[3])

        x_codes = {(g, u): keep.tile([P, S], U32, name="x_codes%d%d" % (g, u), align_bytes=64) for g, u in ((0, 0), (1, 0), (1, 1))}
        x_scales = keep.tile([P, 2, NPICK], U8, name="x_scales", align_bytes=64)

        def pick(i, x_half, j0, j1, picked):
            g, t = divmod(i, PACK)
            nc.vector.tensor_copy(picked, pages[i][:].indirect(idx5[:, j0 // 16 : j1 // 16]))
            for lo in range(j0, j1, S):
                hi = min(lo + S, j1)
                nc.scalar.activation(
                    out=x_half[lo // S][:, lo % S : lo % S + hi - lo, t], in_=picked[:, lo - j0 : hi - j0],
                    func=ACT.Identity, bias=vec_col[:, g, t : t + 1],
                )

        def quantize_x(g, x_half, j0, j1):
            cols = slice(j0 % S, j0 % S + j1 - j0)
            src = x_half[j0 // S][:, cols, :].rearrange("p j t -> p (j t)")
            nc.vector.quantize_mx(out=x_codes[g, j0 // S][:, cols].bitcast(FP8X4), scales=x_scales[:, g, j0:j1], in_=src)

        x0 = [half.tile([P, S, PACK], BF16, name="half", align_bytes=64) for u in range(2)]
        x1 = [half.tile([P, S, PACK], BF16, name="half", align_bytes=64) for u in range(2)]
        h = h2_rows(0, row_tile()[:])
        spent = None
        for i in range(2 * PACK - 1):
            scatter(pages[i], idx4, h, gain2[i % PACK])
            h = h2_rows(i + 1, row_tile()[:] if i < 2 else spent[:, 0:S])
            if i == 0:
                w3q.append(quantize(round_weight(nc.scalar.copy, w3_raw[1])[:], KP, "w3_1"))
                for a in range(2):
                    quantize_w4(a, 1)
            late = i + 2
            if PACK <= late < 2 * PACK:
                scatter(pages[late], idx3, h1_rows(late, spent[:, S:NPICK]), gain1[late % PACK])
            spent = big.tile([P, NPICK], F32, name="big", align_bytes=64)
            pick(i, (x0, x1)[i // PACK], 0, NPICK, spent[:])
            if i == PACK:
                quantize_x(0, x0, 0, S)
        scatter(pages[7], idx4, h, gain2[3])

        CH = 256
        acc = [[bank() for n2 in range(2)] for c in range(4)]

        def final_passes(g, c):
            for n2 in range(2):
                for e in range(4):
                    n, j0 = 2 * n2 + e // 2, CH * c + P * (e % 2)
                    mx(acc[c][n2][:, P * e : P * (e + 1)],
                       w5_w[:, g, 2 * P * n : 2 * P * (n + 1)], w5_plane[:, N * g + P * n : N * g + P * (n + 1)], FP4X4,
                       x_codes[g, j0 // S][:, j0 % S : j0 % S + P], x_scales[:, g, j0 : j0 + P],
                       g == 0 and e == 0, g == 1 and e == 3)

        out_rows = out.rearrange("(n p) j -> p n j", p=P)

        def as_f32(x_tile):
            return x_tile[:].rearrange("p j t -> p (j t)").bitcast(F32)

        def finish(c):
            quantize_x(1, x1, CH * c, CH * (c + 1))
            final_passes(1, c)
            for n2 in range(2):
                res = row_tile()
                (nc.vector.tensor_copy if n2 == 0 else nc.scalar.copy)(out=res[:], in_=acc[c][n2][:])
                nc.sync.dma_start(
                    out=out_rows[:, 2 * n2 : 2 * n2 + 2, CH * c : CH * (c + 1)],
                    in_=res[:].rearrange("p (n j) -> p n j", n=2),
                )

        for c in range(2):
            final_passes(0, c)
        for c in range(4):
            if c == 1:
                picked = pair.tile([P, CH], F32, name="last", align_bytes=64)[:]
            else:
                picked = as_f32(x0[0])[:, CH * c : CH * (c + 1)]
            pick(7, x1, CH * c, CH * (c + 1), picked)
            if c == 1:
                x_codes[0, 1] = pair.tile([P, S], U32, name="last", align_bytes=64)
                quantize_x(0, x0, S, 2 * S)
        finish(0)
        for c in range(2, 4):
            final_passes(0, c)
        for c in range(1, 4):
            finish(c)
